import numpy as np
import ml_dtypes


def mxq(x, axis, fmt="e4m3"):
    dtype, down = {"e4m3": (ml_dtypes.float8_e4m3fn, 7), "e5m2": (ml_dtypes.float8_e5m2, 14)}[fmt]
    v = np.moveaxis(np.asarray(x, np.float32).astype(ml_dtypes.bfloat16).astype(np.float64), axis, -1)
    blocks = v.reshape(v.shape[:-1] + (-1, 32))
    amax = np.abs(blocks).max(-1, keepdims=True)
    byte = np.maximum(np.where(amax > 0, np.frexp(amax)[1] - 1 + 127, 0) - down, 1)
    scale = np.exp2(byte - 127.0)
    codes = (blocks / scale).astype(np.float32).astype(dtype).astype(np.float64)
    return np.moveaxis((codes * scale).reshape(v.shape), -1, axis)


WIDE = False


def mx_kscale(k):
    if not WIDE:
        return np.ones(k)
    levels = np.array([10, -10, 5, -5, 0])
    if k % 512:
        return np.exp2(np.random.permutation(np.resize(levels, k // 32))).repeat(32)
    a = np.empty((k // 512, 16))
    for p in range(k // 512):
        a[p, :8] = np.random.permutation(np.resize(levels, 8))
        for g in range(8):
            far = levels[np.abs(levels - a[p, g]) >= 10]
            a[p, g + 8] = far[np.random.randint(len(far))]
    return np.exp2(a.ravel()).repeat(32)


BF16 = ml_dtypes.bfloat16


def bf(x):
    return np.asarray(x, np.float32).astype(BF16)


def f64(x):
    return np.asarray(x).astype(np.float64)


E2M1 = np.array([0.0, 0.5, 1.0, 1.5, 2.0, 3.0, 4.0, 6.0, -0.0, -0.5, -1.0, -1.5, -2.0, -3.0, -4.0, -6.0])


def pack_weight(w, fmt):
    k, n = w.shape
    w = f64(bf(w)).reshape(k // 32, 32, n)
    amax = np.abs(w).max(1)
    if fmt == "e4m3":
        byte = np.frexp(amax)[1] - 1 + 127 - 7
    else:
        mant, ex = np.frexp(amax / 6.0)
        byte = np.where(mant > 0.5, ex, ex - 1) + 127
    byte = np.clip(np.where(amax > 0, byte, 1), 1, 254)
    scaled = (w * np.exp2(127.0 - byte)[:, None, :]).reshape(k, n).astype(np.float32)
    by_word = np.ascontiguousarray(scaled.reshape(k // 512, 128, 4, n).transpose(0, 1, 3, 2))
    if fmt == "e4m3":
        words = by_word.astype(ml_dtypes.float8_e4m3fn).view(np.uint8)
    else:
        c = by_word.astype(ml_dtypes.float4_e2m1fn).view(np.uint8) & 0xF
        words = c[..., 0::2] | (c[..., 1::2] << 4)
    return np.ascontiguousarray(words), np.ascontiguousarray(byte.astype(np.uint8).reshape(k // 512, 16, n))


def unpack_weight(words, scales, fmt):
    g, p, n, _ = words.shape
    if fmt == "e4m3":
        vals = np.ascontiguousarray(words).view(ml_dtypes.float8_e4m3fn).astype(np.float64)
    else:
        nib = np.empty((g, p, n, 4), np.uint8)
        nib[..., 0::2] = words & 0xF
        nib[..., 1::2] = words >> 4
        vals = E2M1[nib]
    vals = vals * np.repeat(np.exp2(scales.astype(np.float64) - 127.0), 8, axis=1)[..., None]
    return vals.transpose(0, 1, 3, 2).reshape(g * 512, n)
def pack4(w):
    words, scales = pack_weight(w, "e2m1")
    return words.reshape(words.shape[0], 128, -1), scales


def unpack4(words, scales):
    return unpack_weight(words.reshape(words.shape[0], 128, -1, 2), scales, "e2m1")


M, K, R, N = 1024, 1024, 512, 1024


def setup_inputs():
    s = mx_kscale(K)
    t = mx_kscale(R)
    sym = np.random.randint(0, 4, (K, M)) - 1.5
    dig = np.random.standard_normal((K, 2 * R)) / np.sqrt(K)
    theta = np.random.uniform(-np.pi, np.pi, (R, N))
    gain = 1 + 0.1 * np.random.standard_normal(2 * R)
    sym_words, sym_scales = pack4(sym * s[:, None])
    dig_words, dig_scales = pack4(dig / s[:, None])
    return {"sym_words": sym_words, "sym_scales": sym_scales,
            "dig_words": dig_words, "dig_scales": dig_scales,
            "gain": bf(gain * np.concatenate([t, t])),
            "cosw": bf(np.cos(theta) / np.sqrt(R) / t[:, None]),
            "sinw": bf(np.sin(theta) / np.sqrt(R) / t[:, None])}


def reference(sym_words, sym_scales, dig_words, dig_scales, gain, cosw, sinw):
    x = unpack4(sym_words, sym_scales)
    d = unpack4(dig_words, dig_scales)
    h = x.T @ d
    h = np.tanh(h) * f64(gain)
    u = mxq(h[:, :R], 1, "e4m3")
    v = mxq(h[:, R:], 1, "e4m3")
    c = mxq(f64(cosw), 0, "e4m3")
    b = mxq(f64(sinw), 0, "e4m3")
    y_re = (u @ c) - (v @ b)
    y_im = (u @ b) + (v @ c)
    return y_re, y_im

@@ -1,0 +1,247 @@
+from contextlib import ExitStack
+
+import concourse.mybir as mybir
+from concourse.masks import make_identity
+
+FLOPS = 2 * 1024 * 1024 * 1024 + 4 * 2 * 1024 * 512 * 1024
+
+F32 = mybir.dt.float32
+BF16 = mybir.dt.bfloat16
+I32 = mybir.dt.int32
+U32 = mybir.dt.uint32
+U8 = mybir.dt.uint8
+FP4X4 = mybir.dt.float4_e2m1fn_x4
+FP8X4 = mybir.dt.float8_e4m3fn_x4
+TANH = mybir.ActivationFunctionType.Tanh
+MULT = mybir.AluOpType.mult
+
+
+def tile_hybrid_beamforming_precoder_s4_kernel(
+    tc, sym_words, sym_scales, dig_words, dig_scales, gain, cosw, sinw, out_0, out_1
+):
+    nc = tc.nc
+    with ExitStack() as ctx:
+        keep = ctx.enter_context(tc.tile_pool(name="keep", bufs=1))
+        ypool = ctx.enter_context(tc.tile_pool(name="ypool", bufs=16))
+        yfull = ctx.enter_context(tc.tile_pool(name="yfull", bufs=4))
+        psum = ctx.enter_context(tc.psum_pool(name="psum", bufs=8))
+
+        def kt(shape, dtype, name):
+            return keep.tile(shape, dtype, name=name, align_bytes=64)
+
+        d_raw = kt([128, 2, 2048], U8, "d_raw")
+        d_codes = kt([128, 4, 2, 2, 256], U8, "d_codes")
+        ds_raw = kt([128, 2, 1024], U8, "ds_raw")
+        ds = kt([128, 4, 2, 2, 128], U8, "ds")
+        x_codes = kt([128, 2, 2, 1024], U8, "x_codes")
+        xs = kt([128, 2, 1024], U8, "xs")
+        g_rows = kt([128, 128], BF16, "g_rows")
+        ident = kt([128, 128], BF16, "ident")
+        g_sb = kt([128, 8], F32, "g_sb")
+        warm = kt([128, 1], F32, "warm")
+
+        w_raw, w_il, w_codes, w_sc = {}, {}, {}, {}
+        for nh in range(2):
+            for k in ("c", "b"):
+                w_raw[k, nh] = kt([128, 4, 512], BF16, "raw_%s%d" % (k, nh))
+            for k in ("c", "b", "nb"):
+                w_il[k, nh] = kt([128, 2048], BF16, "il_%s%d" % (k, nh))
+                w_codes[k, nh] = kt([128, 512], U32, "wq_%s%d" % (k, nh))
+                w_sc[k, nh] = kt([128, 512], U8, "ws_%s%d" % (k, nh))
+        th, uv_il, uv_codes, uv_sc = {}, {}, {}, {}
+        for s in range(2):
+            for h in range(2):
+                th[s, h] = kt([128, 4, 512], F32, "th_%d%d" % (s, h))
+            for q in range(4):
+                uv_il[s, q] = kt([128, 1024], BF16, "uvil_%d%d" % (s, q))
+                uv_codes[s, q] = kt([128, 256], U32, "uvq_%d%d" % (s, q))
+                uv_sc[s, q] = kt([128, 256], U8, "uvs_%d%d" % (s, q))
+
+        ctx.enter_context(tc.manual_schedule())
+
+        def load_x(eng, h):
+            eng.dma_start(
+                out=x_codes[:, :, h, :].bitcast(I32),
+                in_=sym_words.rearrange("g p x -> p g x")[:, :, h * 1024 : (h + 1) * 1024].bitcast(I32),
+            )
+
+        def load_scales(eng, dst, src, quad):
+            eng.dma_start(
+                out=dst[32 * quad : 32 * quad + 4, :, :].bitcast(I32),
+                in_=src[:, 4 * quad : 4 * quad + 4, :].rearrange("g q n -> q g n").bitcast(I32),
+            )
+
+        def load_w(eng, k, nh):
+            w = (cosw if k == "c" else sinw).rearrange("(b t i) n -> i b t n", t=4, i=4)
+            for i in range(4):
+                eng.dma_start(out=w_raw[k, nh][i:128:4, :, :], in_=w[i][:, :, nh * 512 : (nh + 1) * 512])
+
+        nc.vector.memset(ds_raw[:].rearrange("p g n -> p (g n)").bitcast(I32), 0)
+        nc.vector.memset(xs[:].rearrange("p g n -> p (g n)").bitcast(I32), 0)
+        for quad in range(4):
+            load_scales(nc.scalar, ds_raw, dig_scales, quad)
+        for quad in range(4):
+            load_scales(nc.scalar if quad < 2 else nc.gpsimd, xs, sym_scales, quad)
+        nc.sync.dma_start(out=d_raw[:].bitcast(I32), in_=dig_words.rearrange("g p x -> p g x").bitcast(I32))
+        load_x(nc.sync, 0)
+        nc.gpsimd.memset(warm[:], 0.0)
+        nc.gpsimd.memset(g_rows[:], 0.0)
+        make_identity(nc, ident[:])
+        nc.scalar.activation(out=warm[:], in_=warm[:], func=TANH)
+
+        load_w(nc.sync, "c", 0)
+        load_w(nc.sync, "b", 0)
+        g_src = gain.rearrange("(s b t i) -> s t b i", s=2, t=4, i=4)
+        for s in range(2):
+            nc.sync.dma_start(
+                out=g_rows[4 * s : 4 * s + 4, :].rearrange("t (b i) -> t b i", i=4), in_=g_src[s]
+            )
+        load_x(nc.sync, 1)
+        load_w(nc.sync, "c", 1)
+        load_w(nc.sync, "b", 1)
+
+        nc.vector.tensor_copy(
+            out=ds[:].rearrange("p t g s n -> p (t g s n)").bitcast(I32).rearrange("p (t c) -> p t c", t=4),
+            in_=ds_raw[:].rearrange("p g n -> p (g n)").bitcast(I32).rearrange("p (c t) -> p t c", t=4),
+        )
+        d_dst = d_codes[:].rearrange("p t g s n -> p (t g s n)").bitcast(I32).rearrange("p (t g c w) -> p g t c w", t=4, g=2, w=2)
+        d_src = d_raw[:].rearrange("p g x -> p (g x)").bitcast(I32).rearrange("p (g c t w) -> p g t c w", g=2, t=4, w=2)
+        for g in range(2):
+            nc.vector.tensor_copy(out=d_dst[:, g], in_=d_src[:, g])
+
+        def stage1(s, t, n0, width):
+            h, r = n0 // 512, n0 % 512
+            bank = psum.tile([128, width], F32, name="bank")
+            for g in range(2):
+                nc.tensor.matmul_mx(
+                    out=bank[:],
+                    lhsT=d_codes[:, t, g, s, :].bitcast(FP4X4),
+                    lhsT_scale=ds[:, t, g, s, :],
+                    rhs=x_codes[:, g, h, 2 * r : 2 * (r + width)].bitcast(FP4X4),
+                    rhs_scale=xs[:, g, n0 : n0 + width],
+                    start=(g == 0),
+                    stop=(g == 1),
+                )
+            nc.scalar.activation(out=th[s, h][:, t, r : r + width], in_=bank[:], func=TANH)
+
+        def interleave_w(k, nh):
+            nc.vector.tensor_copy(
+                out=w_il[k, nh][:].rearrange("p (c i t) -> p c t i", i=4, t=4),
+                in_=w_raw[k, nh][:].rearrange("p t (c i) -> p c t i", i=4),
+            )
+
+        def negate_b(nh):
+            nc.vector.tensor_scalar(out=w_il["nb", nh][:], in0=w_il["b", nh][:], scalar1=-1.0, scalar2=None, op0=MULT)
+
+        def quant_w(k, nh):
+            nc.vector.quantize_mx(out=w_codes[k, nh][:].bitcast(FP8X4), scales=w_sc[k, nh][:], in_=w_il[k, nh][:])
+
+        def mul_gain(s, q):
+            h, r = q // 2, q % 2
+            nc.vector.tensor_tensor(
+                out=uv_il[s, q][:].rearrange("p (c i t) -> p c t i", i=4, t=4),
+                in0=th[s, h][:, :, r * 256 : (r + 1) * 256].rearrange("p t (c i) -> p c t i", i=4),
+                in1=g_sb[:, 4 * s : 4 * s + 4].unsqueeze(1).unsqueeze(3).to_broadcast([128, 64, 4, 4]),
+                op=MULT,
+            )
+
+        def quant_uv(s, q):
+            nc.vector.quantize_mx(out=uv_codes[s, q][:].bitcast(FP8X4), scales=uv_sc[s, q][:], in_=uv_il[s, q][:])
+
+        def mm2(bank, s, m, k, nh, start, stop):
+            q, r = m // 2, m % 2
+            nc.tensor.matmul_mx(
+                out=bank[:],
+                lhsT=uv_codes[s, q][:, r * 128 : (r + 1) * 128].bitcast(FP8X4),
+                lhsT_scale=uv_sc[s, q][:, r * 128 : (r + 1) * 128],
+                rhs=w_codes[k, nh][:].bitcast(FP8X4),
+                rhs_scale=w_sc[k, nh][:],
+                start=start,
+                stop=stop,
+            )
+
+        def group(m, nh, ri, y, ycol, eng):
+            bank = psum.tile([128, 512], F32, name="bank")
+            ks = ("c", "nb") if ri == 0 else ("b", "c")
+            mm2(bank, 0, m, ks[0], nh, True, False)
+            mm2(bank, 1, m, ks[1], nh, False, True)
+            if eng == "s":
+                nc.scalar.copy(out=y[:, ycol : ycol + 512], in_=bank[:])
+            else:
+                nc.vector.tensor_copy(out=y[:, ycol : ycol + 512], in_=bank[:])
+
+        def store(m, ri, y, n0, width):
+            out = (out_0, out_1)[ri]
+            nc.sync.dma_start(out=out[m * 128 : (m + 1) * 128, n0 : n0 + width], in_=y[:])
+
+        def half_rows(m, nh, ri, eng):
+            y = ypool.tile([128, 512], F32, name="yh")
+            group(m, nh, ri, y, 0, eng)
+            store(m, ri, y, nh * 512, 512)
+
+        def full_rows(m, ri, engs):
+            y = yfull.tile([128, 1024], F32, name="yf")
+            group(m, 0, ri, y, 0, engs[0])
+            group(m, 1, ri, y, 512, engs[1])
+            store(m, ri, y, 0, 1024)
+
+        for s in range(2):
+            for t in range(4):
+                stage1(s, t, 0, 256)
+        g_ps = psum.tile([128, 128], BF16, name="bank")
+        nc.tensor.transpose(g_ps[:], g_rows[:], ident[:])
+        for s in range(2):
+            for t in range(4):
+                stage1(s, t, 256, 256)
+        for t in range(3):
+            stage1(0, t, 512, 512)
+
+        interleave_w("c", 0)
+        interleave_w("b", 0)
+        quant_w("c", 0)
+        quant_w("b", 0)
+        nc.vector.tensor_copy(out=g_sb[:], in_=g_ps[:, 0:8])
+        mul_gain(0, 0)
+        mul_gain(1, 0)
+        quant_uv(0, 0)
+        quant_uv(1, 0)
+        negate_b(0)
+        quant_w("nb", 0)
+        for ri in (1, 0):
+            for m in (0, 1):
+                half_rows(m, 0, ri, "s")
+        mul_gain(0, 1)
+        mul_gain(1, 1)
+        quant_uv(0, 1)
+        quant_uv(1, 1)
+        stage1(0, 3, 512, 512)
+        stage1(1, 0, 512, 512)
+        for ri in (1, 0):
+            for m in (2, 3):
+                half_rows(m, 0, ri, "s")
+        for t in (1, 2, 3):
+            stage1(1, t, 512, 512)
+        interleave_w("c", 1)
+        interleave_w("b", 1)
+        quant_w("c", 1)
+        quant_w("b", 1)
+        mul_gain(0, 2)
+        negate_b(1)
+        mul_gain(1, 2)
+        quant_w("nb", 1)
+        quant_uv(0, 2)
+        quant_uv(1, 2)
+        for ri in (1, 0):
+            for m in range(4):
+                half_rows(m, 1, ri, "s")
+        mul_gain(0, 3)
+        mul_gain(1, 3)
+        quant_uv(0, 3)
+        quant_uv(1, 3)
+        for m in range(4, 8):
+            for ri in range(2):
+                if m < 7 or ri < 1:
+                    full_rows(m, ri, "ss" if m == 4 else "vs")
+                else:
+                    half_rows(m, 0, ri, "v")
+                    half_rows(m, 1, ri, "s")

@@ -37,7 +37,7 @@ def tile_hybrid_beamforming_precoder_s4_kernel(
         xs = kt([128, 2, 1024], U8, "xs")
         g_rows = kt([128, 128], BF16, "g_rows")
         ident = kt([128, 128], BF16, "ident")
-        g_sb = kt([128, 8], F32, "g_sb")
+        g_sb = kt([128, 2, 4, 2], F32, "g_sb")
         warm = kt([128, 1], F32, "warm")
 
         w_raw, w_il, w_codes, w_sc = {}, {}, {}, {}
@@ -77,7 +77,7 @@ def tile_hybrid_beamforming_precoder_s4_kernel(
                 eng.dma_start(out=w_raw[k, nh][i:128:4, :, :], in_=w[i][:, :, nh * 512 : (nh + 1) * 512])
 
         nc.vector.memset(ds_raw[:].rearrange("p g n -> p (g n)").bitcast(I32), 0)
-        nc.vector.memset(xs[:].rearrange("p g n -> p (g n)").bitcast(I32), 0)
+        nc.gpsimd.memset(xs[:].rearrange("p g n -> p (g n)").bitcast(I32), 0)
         for quad in range(4):
             load_scales(nc.scalar, ds_raw, dig_scales, quad)
         for quad in range(4):
@@ -139,9 +139,9 @@ def tile_hybrid_beamforming_precoder_s4_kernel(
         def mul_gain(s, q):
             h, r = q // 2, q % 2
             nc.vector.tensor_tensor(
-                out=uv_il[s, q][:].rearrange("p (c i t) -> p c t i", i=4, t=4),
-                in0=th[s, h][:, :, r * 256 : (r + 1) * 256].rearrange("p t (c i) -> p c t i", i=4),
-                in1=g_sb[:, 4 * s : 4 * s + 4].unsqueeze(1).unsqueeze(3).to_broadcast([128, 64, 4, 4]),
+                out=uv_il[s, q][:].rearrange("p (c i t) -> p c t i", i=2, t=4),
+                in0=th[s, h][:, :, r * 256 : (r + 1) * 256].rearrange("p t (c i) -> p c t i", i=2),
+                in1=g_sb[:, s, :, :].unsqueeze(1).to_broadcast([128, 128, 4, 2]),
                 op=MULT,
             )
 
@@ -200,7 +200,9 @@ def tile_hybrid_beamforming_precoder_s4_kernel(
         interleave_w("b", 0)
         quant_w("c", 0)
         quant_w("b", 0)
-        nc.vector.tensor_copy(out=g_sb[:], in_=g_ps[:, 0:8])
+        nc.vector.tensor_copy(
+            out=g_sb[:].rearrange("p s t i -> p (s t) i"), in_=g_ps[:, 0:8].unsqueeze(2).to_broadcast([128, 8, 2])
+        )
         mul_gain(0, 0)
         mul_gain(1, 0)
         quant_uv(0, 0)

@@ -22,8 +22,8 @@ def tile_hybrid_beamforming_precoder_s4_kernel(
     nc = tc.nc
     with ExitStack() as ctx:
         keep = ctx.enter_context(tc.tile_pool(name="keep", bufs=1))
-        ypool = ctx.enter_context(tc.tile_pool(name="ypool", bufs=16))
-        yfull = ctx.enter_context(tc.tile_pool(name="yfull", bufs=4))
+        ypool = ctx.enter_context(tc.tile_pool(name="ypool", bufs=6))
+        yfull = ctx.enter_context(tc.tile_pool(name="yfull", bufs=14))
         psum = ctx.enter_context(tc.psum_pool(name="psum", bufs=8))
 
         def kt(shape, dtype, name):
@@ -37,7 +37,7 @@ def tile_hybrid_beamforming_precoder_s4_kernel(
         xs = kt([128, 2, 1024], U8, "xs")
         g_rows = kt([128, 128], BF16, "g_rows")
         ident = kt([128, 128], BF16, "ident")
-        g_sb = kt([128, 2, 4, 2], F32, "g_sb")
+        g_sb = kt([128, 8], F32, "g_sb")
         warm = kt([128, 1], F32, "warm")
 
         w_raw, w_il, w_codes, w_sc = {}, {}, {}, {}
@@ -48,14 +48,15 @@ def tile_hybrid_beamforming_precoder_s4_kernel(
                 w_il[k, nh] = kt([128, 2048], BF16, "il_%s%d" % (k, nh))
                 w_codes[k, nh] = kt([128, 512], U32, "wq_%s%d" % (k, nh))
                 w_sc[k, nh] = kt([128, 512], U8, "ws_%s%d" % (k, nh))
-        th, uv_il, uv_codes, uv_sc = {}, {}, {}, {}
+        th, ub, uv_il, uv_codes, uv_sc = {}, {}, {}, {}, {}
         for s in range(2):
             for h in range(2):
                 th[s, h] = kt([128, 4, 512], F32, "th_%d%d" % (s, h))
-            for q in range(4):
-                uv_il[s, q] = kt([128, 1024], BF16, "uvil_%d%d" % (s, q))
-                uv_codes[s, q] = kt([128, 256], U32, "uvq_%d%d" % (s, q))
-                uv_sc[s, q] = kt([128, 256], U8, "uvs_%d%d" % (s, q))
+                ub[s, h] = kt([128, 4, 512], BF16, "ub_%d%d" % (s, h))
+            for m in range(8):
+                uv_il[s, m] = kt([128, 512], BF16, "uvil_%d%d" % (s, m))
+                uv_codes[s, m] = kt([128, 128], U32, "uvq_%d%d" % (s, m))
+                uv_sc[s, m] = kt([128, 128], U8, "uvs_%d%d" % (s, m))
 
         ctx.enter_context(tc.manual_schedule())
 
@@ -76,26 +77,26 @@ def tile_hybrid_beamforming_precoder_s4_kernel(
             for i in range(4):
                 eng.dma_start(out=w_raw[k, nh][i:128:4, :, :], in_=w[i][:, :, nh * 512 : (nh + 1) * 512])
 
+        nc.gpsimd.dma_start(out=d_raw[:].bitcast(I32), in_=dig_words.rearrange("g p x -> p g x").bitcast(I32))
+        load_x(nc.gpsimd, 0)
         nc.vector.memset(ds_raw[:].rearrange("p g n -> p (g n)").bitcast(I32), 0)
-        nc.gpsimd.memset(xs[:].rearrange("p g n -> p (g n)").bitcast(I32), 0)
+        nc.vector.memset(xs[:].rearrange("p g n -> p (g n)").bitcast(I32), 0)
         for quad in range(4):
             load_scales(nc.scalar, ds_raw, dig_scales, quad)
         for quad in range(4):
-            load_scales(nc.scalar if quad < 2 else nc.gpsimd, xs, sym_scales, quad)
-        nc.sync.dma_start(out=d_raw[:].bitcast(I32), in_=dig_words.rearrange("g p x -> p g x").bitcast(I32))
-        load_x(nc.sync, 0)
-        nc.gpsimd.memset(warm[:], 0.0)
-        nc.gpsimd.memset(g_rows[:], 0.0)
+            load_scales(nc.sync, xs, sym_scales, quad)
+        load_w(nc.gpsimd, "c", 0)
+        nc.vector.memset(g_rows[:], 0.0)
+        nc.vector.memset(warm[:], 0.0)
+        g_src = gain.rearrange("(s b t i) -> s t b i", s=2, t=4, i=4)
+        for s in range(2):
+            nc.gpsimd.dma_start(
+                out=g_rows[4 * s : 4 * s + 4, :].rearrange("t (b i) -> t b i", i=4), in_=g_src[s]
+            )
         make_identity(nc, ident[:])
         nc.scalar.activation(out=warm[:], in_=warm[:], func=TANH)
 
-        load_w(nc.sync, "c", 0)
         load_w(nc.sync, "b", 0)
-        g_src = gain.rearrange("(s b t i) -> s t b i", s=2, t=4, i=4)
-        for s in range(2):
-            nc.sync.dma_start(
-                out=g_rows[4 * s : 4 * s + 4, :].rearrange("t (b i) -> t b i", i=4), in_=g_src[s]
-            )
         load_x(nc.sync, 1)
         load_w(nc.sync, "c", 1)
         load_w(nc.sync, "b", 1)
@@ -124,38 +125,62 @@ def tile_hybrid_beamforming_precoder_s4_kernel(
                 )
             nc.scalar.activation(out=th[s, h][:, t, r : r + width], in_=bank[:], func=TANH)
 
-        def interleave_w(k, nh):
+        def cols(nh, part):
+            return slice(0, 512) if part is None else slice(256 * part, 256 * part + 256)
+
+        def interleave_w(k, nh, part=None, eng="v"):
+            c = cols(nh, part)
+            dst = w_il[k, nh][:].rearrange("p (n t) -> p n t", t=4)[:, c, :]
+            src = w_raw[k, nh][:, :, c].rearrange("p t n -> p n t")
+            if eng == "v":
+                nc.vector.tensor_copy(out=dst, in_=src)
+            else:
+                nc.scalar.copy(out=dst, in_=src)
+
+        def negate_b(nh, part=None):
+            c = cols(nh, part)
+            c4 = slice(4 * c.start, 4 * c.stop)
+            nc.vector.tensor_scalar(
+                out=w_il["nb", nh][:, c4], in0=w_il["b", nh][:, c4], scalar1=-1.0, scalar2=None, op0=MULT
+            )
+
+        def quant_w(k, nh, part=None):
+            c = cols(nh, part)
+            nc.vector.quantize_mx(
+                out=w_codes[k, nh][:, c].bitcast(FP8X4),
+                scales=w_sc[k, nh][:, c],
+                in_=w_il[k, nh][:, 4 * c.start : 4 * c.stop],
+            )
+
+        def mul_gain(s, n0, width):
+            h, r = n0 // 512, n0 % 512
+            for t in range(4):
+                nc.vector.tensor_scalar(
+                    out=ub[s, h][:, t, r : r + width],
+                    in0=th[s, h][:, t, r : r + width],
+                    scalar1=g_sb[:, 4 * s + t : 4 * s + t + 1],
+                    scalar2=None,
+                    op0=MULT,
+                )
+
+        def interleave_uv(s, m):
+            h, r = m // 4, 128 * (m % 4)
             nc.vector.tensor_copy(
-                out=w_il[k, nh][:].rearrange("p (c i t) -> p c t i", i=4, t=4),
-                in_=w_raw[k, nh][:].rearrange("p t (c i) -> p c t i", i=4),
+                out=uv_il[s, m][:].rearrange("p (n t) -> p n t", t=4),
+                in_=ub[s, h][:, :, r : r + 128].rearrange("p t n -> p n t"),
             )
 
-        def negate_b(nh):
-            nc.vector.tensor_scalar(out=w_il["nb", nh][:], in0=w_il["b", nh][:], scalar1=-1.0, scalar2=None, op0=MULT)
+        def quant_uv(s, m):
+            nc.vector.quantize_mx(out=uv_codes[s, m][:].bitcast(FP8X4), scales=uv_sc[s, m][:], in_=uv_il[s, m][:])
 
-        def quant_w(k, nh):
-            nc.vector.quantize_mx(out=w_codes[k, nh][:].bitcast(FP8X4), scales=w_sc[k, nh][:], in_=w_il[k, nh][:])
-
-        def mul_gain(s, q):
-            h, r = q // 2, q % 2
-            nc.vector.tensor_tensor(
-                out=uv_il[s, q][:].rearrange("p (c i t) -> p c t i", i=2, t=4),
-                in0=th[s, h][:, :, r * 256 : (r + 1) * 256].rearrange("p t (c i) -> p c t i", i=2),
-                in1=g_sb[:, s, :, :].unsqueeze(1).to_broadcast([128, 128, 4, 2]),
-                op=MULT,
-            )
-
-        def quant_uv(s, q):
-            nc.vector.quantize_mx(out=uv_codes[s, q][:].bitcast(FP8X4), scales=uv_sc[s, q][:], in_=uv_il[s, q][:])
-
-        def mm2(bank, s, m, k, nh, start, stop):
-            q, r = m // 2, m % 2
+        def mm2(bank, s, m, k, nh, start, stop, part=None):
+            c = cols(nh, part)
             nc.tensor.matmul_mx(
-                out=bank[:],
-                lhsT=uv_codes[s, q][:, r * 128 : (r + 1) * 128].bitcast(FP8X4),
-                lhsT_scale=uv_sc[s, q][:, r * 128 : (r + 1) * 128],
-                rhs=w_codes[k, nh][:].bitcast(FP8X4),
-                rhs_scale=w_sc[k, nh][:],
+                out=bank,
+                lhsT=uv_codes[s, m][:].bitcast(FP8X4),
+                lhsT_scale=uv_sc[s, m][:],
+                rhs=w_codes[k, nh][:, c].bitcast(FP8X4),
+                rhs_scale=w_sc[k, nh][:, c],
                 start=start,
                 stop=stop,
             )
@@ -163,8 +188,8 @@ def tile_hybrid_beamforming_precoder_s4_kernel(
         def group(m, nh, ri, y, ycol, eng):
             bank = psum.tile([128, 512], F32, name="bank")
             ks = ("c", "nb") if ri == 0 else ("b", "c")
-            mm2(bank, 0, m, ks[0], nh, True, False)
-            mm2(bank, 1, m, ks[1], nh, False, True)
+            mm2(bank[:], 0, m, ks[0], nh, True, False)
+            mm2(bank[:], 1, m, ks[1], nh, False, True)
             if eng == "s":
                 nc.scalar.copy(out=y[:, ycol : ycol + 512], in_=bank[:])
             else:
@@ -185,65 +210,73 @@ def tile_hybrid_beamforming_precoder_s4_kernel(
             group(m, 1, ri, y, 512, engs[1])
             store(m, ri, y, 0, 1024)
 
-        for s in range(2):
-            for t in range(4):
-                stage1(s, t, 0, 256)
-        g_ps = psum.tile([128, 128], BF16, name="bank")
-        nc.tensor.transpose(g_ps[:], g_rows[:], ident[:])
-        for s in range(2):
-            for t in range(4):
-                stage1(s, t, 256, 256)
-        for t in range(3):
-            stage1(0, t, 512, 512)
+        def quarter(m, part, y):
+            bank = psum.tile([128, 2, 256], F32, name="bank")
+            for ri, ks in ((1, ("b", "c")), (0, ("c", "nb"))):
+                for s in range(2):
+                    mm2(bank[:, ri, :], s, m, ks[s], 1, s == 0, s == 1, part)
+            nc.scalar.copy(out=y[:, :, 256 * part : 256 * part + 256], in_=bank[:])
+
+        def samples(m):
+            interleave_uv(0, m)
+            interleave_uv(1, m)
+            quant_uv(0, m)
+            quant_uv(1, m)
+
+        for n0 in (0, 256):
+            for s in range(2):
+                for t in range(4):
+                    stage1(s, t, n0, 256)
+            if n0 == 0:
+                g_ps = psum.tile([128, 128], BF16, name="bank")
+                nc.tensor.transpose(g_ps[:], g_rows[:], ident[:])
+        interleave_w("c", 1, None, "s")
+        stage1(0, 0, 512, 512)
+        stage1(0, 1, 512, 512)
 
         interleave_w("c", 0)
         interleave_w("b", 0)
         quant_w("c", 0)
+        nc.vector.tensor_copy(out=g_sb[:], in_=g_ps[:, 0:8])
         quant_w("b", 0)
-        nc.vector.tensor_copy(
-            out=g_sb[:].rearrange("p s t i -> p (s t) i"), in_=g_ps[:, 0:8].unsqueeze(2).to_broadcast([128, 8, 2])
-        )
-        mul_gain(0, 0)
-        mul_gain(1, 0)
-        quant_uv(0, 0)
-        quant_uv(1, 0)
+        mul_gain(0, 0, 256)
+        mul_gain(1, 0, 256)
+        samples(0)
+        half_rows(0, 0, 1, "s")
         negate_b(0)
+        mul_gain(0, 256, 256)
         quant_w("nb", 0)
-        for ri in (1, 0):
-            for m in (0, 1):
-                half_rows(m, 0, ri, "s")
-        mul_gain(0, 1)
-        mul_gain(1, 1)
-        quant_uv(0, 1)
-        quant_uv(1, 1)
-        stage1(0, 3, 512, 512)
-        stage1(1, 0, 512, 512)
-        for ri in (1, 0):
-            for m in (2, 3):
-                half_rows(m, 0, ri, "s")
-        for t in (1, 2, 3):
+        half_rows(0, 0, 0, "s")
+        for t in (2, 3):
+            stage1(0, t, 512, 512)
+        for t in (0, 1):
             stage1(1, t, 512, 512)
-        interleave_w("c", 1)
         interleave_w("b", 1)
         quant_w("c", 1)
         quant_w("b", 1)
-        mul_gain(0, 2)
         negate_b(1)
-        mul_gain(1, 2)
+        interleave_uv(0, 1)
         quant_w("nb", 1)
-        quant_uv(0, 2)
-        quant_uv(1, 2)
-        for ri in (1, 0):
-            for m in range(4):
-                half_rows(m, 1, ri, "s")
-        mul_gain(0, 3)
-        mul_gain(1, 3)
-        quant_uv(0, 3)
-        quant_uv(1, 3)
+        half_rows(0, 1, 1, "s")
+        half_rows(0, 1, 0, "s")
+        interleave_uv(1, 1)
+        quant_uv(0, 1)
+        quant_uv(1, 1)
+        mul_gain(1, 256, 256)
+        full_rows(1, 1, "ss")
+        full_rows(1, 0, "ss")
+        for t in (2, 3):
+            stage1(1, t, 512, 512)
+        samples(2)
+        samples(3)
+        mul_gain(0, 512, 512)
+        mul_gain(1, 512, 512)
         for m in range(4, 8):
-            for ri in range(2):
-                if m < 7 or ri < 1:
-                    full_rows(m, ri, "ss" if m == 4 else "vs")
+            samples(m)
+        for m in range(2, 8):
+            for ri in (1, 0):
+                if m < 7 or ri > 0:
+                    full_rows(m, ri, "ss" if m < 5 else "vs")
                 else:
                     half_rows(m, 0, ri, "v")
                     half_rows(m, 1, ri, "s")

@@ -14,6 +14,8 @@ FP4X4 = mybir.dt.float4_e2m1fn_x4
 FP8X4 = mybir.dt.float8_e4m3fn_x4
 TANH = mybir.ActivationFunctionType.Tanh
 MULT = mybir.AluOpType.mult
+WARM = 8
+VFROM = 5
 
 
 def tile_hybrid_beamforming_precoder_s4_kernel(
@@ -22,37 +24,34 @@ def tile_hybrid_beamforming_precoder_s4_kernel(
     nc = tc.nc
     with ExitStack() as ctx:
         keep = ctx.enter_context(tc.tile_pool(name="keep", bufs=1))
-        ypool = ctx.enter_context(tc.tile_pool(name="ypool", bufs=6))
-        yfull = ctx.enter_context(tc.tile_pool(name="yfull", bufs=14))
+        ypool = ctx.enter_context(tc.tile_pool(name="ypool", bufs=16))
         psum = ctx.enter_context(tc.psum_pool(name="psum", bufs=8))
 
         def kt(shape, dtype, name):
             return keep.tile(shape, dtype, name=name, align_bytes=64)
 
         d_raw = kt([128, 2, 2048], U8, "d_raw")
-        d_codes = kt([128, 4, 2, 2, 256], U8, "d_codes")
+        d_codes = {s: kt([128, 4, 2, 256], U8, "d_codes%d" % s) for s in range(2)}
         ds_raw = kt([128, 2, 1024], U8, "ds_raw")
         ds = kt([128, 4, 2, 2, 128], U8, "ds")
-        x_codes = kt([128, 2, 2, 1024], U8, "x_codes")
+        x_codes = {h: kt([128, 2, 1024], U8, "x_codes%d" % h) for h in range(2)}
         xs = kt([128, 2, 1024], U8, "xs")
-        g_rows = kt([128, 128], BF16, "g_rows")
+        g_rows = kt([128, 2, 128], BF16, "g_rows")
         ident = kt([128, 128], BF16, "ident")
-        g_sb = kt([128, 8], F32, "g_sb")
+        g_sb = kt([128, 2, 4, 2], F32, "g_sb")
         warm = kt([128, 1], F32, "warm")
 
         w_raw, w_il, w_codes, w_sc = {}, {}, {}, {}
-        for nh in range(2):
-            for k in ("c", "b"):
-                w_raw[k, nh] = kt([128, 4, 512], BF16, "raw_%s%d" % (k, nh))
-            for k in ("c", "b", "nb"):
-                w_il[k, nh] = kt([128, 2048], BF16, "il_%s%d" % (k, nh))
-                w_codes[k, nh] = kt([128, 512], U32, "wq_%s%d" % (k, nh))
-                w_sc[k, nh] = kt([128, 512], U8, "ws_%s%d" % (k, nh))
-        th, ub, uv_il, uv_codes, uv_sc = {}, {}, {}, {}, {}
+        for k in ("c", "b"):
+            w_raw[k] = kt([128, 4, 1024], BF16, "raw_" + k)
+        for k in ("c", "b", "nb"):
+            w_il[k] = kt([128, 4096], BF16, "il_" + k)
+            w_codes[k] = kt([128, 1024], U32, "wq_" + k)
+            w_sc[k] = kt([128, 1024], U8, "ws_" + k)
+        th, uv_il, uv_codes, uv_sc = {}, {}, {}, {}
         for s in range(2):
             for h in range(2):
                 th[s, h] = kt([128, 4, 512], F32, "th_%d%d" % (s, h))
-                ub[s, h] = kt([128, 4, 512], BF16, "ub_%d%d" % (s, h))
             for m in range(8):
                 uv_il[s, m] = kt([128, 512], BF16, "uvil_%d%d" % (s, m))
                 uv_codes[s, m] = kt([128, 128], U32, "uvq_%d%d" % (s, m))
@@ -60,9 +59,12 @@ def tile_hybrid_beamforming_precoder_s4_kernel(
 
         ctx.enter_context(tc.manual_schedule())
 
+        def flat_i32(t, pattern):
+            return t[:].rearrange(pattern).bitcast(I32)
+
         def load_x(eng, h):
             eng.dma_start(
-                out=x_codes[:, :, h, :].bitcast(I32),
+                out=x_codes[h][:].bitcast(I32),
                 in_=sym_words.rearrange("g p x -> p g x")[:, :, h * 1024 : (h + 1) * 1024].bitcast(I32),
             )
 
@@ -72,211 +74,187 @@ def tile_hybrid_beamforming_precoder_s4_kernel(
                 in_=src[:, 4 * quad : 4 * quad + 4, :].rearrange("g q n -> q g n").bitcast(I32),
             )
 
-        def load_w(eng, k, nh):
+        def load_w(eng, k):
             w = (cosw if k == "c" else sinw).rearrange("(b t i) n -> i b t n", t=4, i=4)
             for i in range(4):
-                eng.dma_start(out=w_raw[k, nh][i:128:4, :, :], in_=w[i][:, :, nh * 512 : (nh + 1) * 512])
+                eng.dma_start(out=w_raw[k][i:128:4, :, :], in_=w[i])
 
-        nc.gpsimd.dma_start(out=d_raw[:].bitcast(I32), in_=dig_words.rearrange("g p x -> p g x").bitcast(I32))
-        load_x(nc.gpsimd, 0)
-        nc.vector.memset(ds_raw[:].rearrange("p g n -> p (g n)").bitcast(I32), 0)
-        nc.vector.memset(xs[:].rearrange("p g n -> p (g n)").bitcast(I32), 0)
+        nc.vector.memset(flat_i32(ds_raw, "p g n -> p (g n)"), 0)
+        nc.vector.memset(flat_i32(xs, "p g n -> p (g n)"), 0)
+        nc.vector.memset(g_rows[:], 0.0)
+        nc.vector.memset(flat_i32(ds, "p t g s n -> p (t g s n)"), 0)
+        nc.vector.memset(x_codes[1][:, 0, :].bitcast(I32), 0)
+        nc.vector.memset(warm[:], 0.0)
+        ds_flat = ds[:].rearrange("p t g s n -> p (t g s n)")
+        warm_bank = psum.tile([128, 512], F32, name="bank")
+        for k in range(WARM):
+            nc.tensor.matmul_mx(
+                out=warm_bank[:],
+                lhsT=x_codes[1][:, 0, 0:256].bitcast(FP4X4),
+                lhsT_scale=ds_flat[:, 0:128],
+                rhs=x_codes[1][:, 0, :].bitcast(FP4X4),
+                rhs_scale=ds_flat[:, 512:1024],
+                start=True,
+                stop=True,
+            )
+        nc.sync.dma_start(out=d_raw[:].bitcast(I32), in_=dig_words.rearrange("g p x -> p g x").bitcast(I32))
+        load_x(nc.sync, 0)
         for quad in range(4):
             load_scales(nc.scalar, ds_raw, dig_scales, quad)
         for quad in range(4):
-            load_scales(nc.sync, xs, sym_scales, quad)
-        load_w(nc.gpsimd, "c", 0)
-        nc.vector.memset(g_rows[:], 0.0)
-        nc.vector.memset(warm[:], 0.0)
-        g_src = gain.rearrange("(s b t i) -> s t b i", s=2, t=4, i=4)
-        for s in range(2):
-            nc.gpsimd.dma_start(
-                out=g_rows[4 * s : 4 * s + 4, :].rearrange("t (b i) -> t b i", i=4), in_=g_src[s]
-            )
+            load_scales(nc.scalar if quad < 2 else nc.gpsimd, xs, sym_scales, quad)
+        nc.gpsimd.dma_start(
+            out=g_rows[0:4, :, :].rearrange("t s (b i) -> t (s b) i", i=4),
+            in_=gain.rearrange("(c t i) -> t c i", t=4, i=4),
+        )
         make_identity(nc, ident[:])
         nc.scalar.activation(out=warm[:], in_=warm[:], func=TANH)
-
-        load_w(nc.sync, "b", 0)
+        load_w(nc.sync, "c")
+        load_w(nc.sync, "b")
         load_x(nc.sync, 1)
-        load_w(nc.sync, "c", 1)
-        load_w(nc.sync, "b", 1)
 
         nc.vector.tensor_copy(
-            out=ds[:].rearrange("p t g s n -> p (t g s n)").bitcast(I32).rearrange("p (t c) -> p t c", t=4),
-            in_=ds_raw[:].rearrange("p g n -> p (g n)").bitcast(I32).rearrange("p (c t) -> p t c", t=4),
+            out=flat_i32(ds, "p t g s n -> p (t g s n)").rearrange("p (t c) -> p t c", t=4),
+            in_=flat_i32(ds_raw, "p g n -> p (g n)").rearrange("p (c t) -> p t c", t=4),
         )
-        d_dst = d_codes[:].rearrange("p t g s n -> p (t g s n)").bitcast(I32).rearrange("p (t g c w) -> p g t c w", t=4, g=2, w=2)
-        d_src = d_raw[:].rearrange("p g x -> p (g x)").bitcast(I32).rearrange("p (g c t w) -> p g t c w", g=2, t=4, w=2)
-        for g in range(2):
-            nc.vector.tensor_copy(out=d_dst[:, g], in_=d_src[:, g])
+        d_src = flat_i32(d_raw, "p g x -> p (g x)").rearrange("p (g s c t w) -> p g s t c w", g=2, s=2, t=4, w=2)
+        for s in range(2):
+            d_dst = flat_i32(d_codes[s], "p t g n -> p (t g n)").rearrange("p (t g c w) -> p g t c w", t=4, g=2, w=2)
+            for g in range(2):
+                nc.vector.tensor_copy(out=d_dst[:, g], in_=d_src[:, g, s])
 
-        def stage1(s, t, n0, width):
-            h, r = n0 // 512, n0 % 512
-            bank = psum.tile([128, width], F32, name="bank")
+        def stage1(s, t, h):
+            bank = psum.tile([128, 512], F32, name="bank")
             for g in range(2):
                 nc.tensor.matmul_mx(
                     out=bank[:],
-                    lhsT=d_codes[:, t, g, s, :].bitcast(FP4X4),
+                    lhsT=d_codes[s][:, t, g, :].bitcast(FP4X4),
                     lhsT_scale=ds[:, t, g, s, :],
-                    rhs=x_codes[:, g, h, 2 * r : 2 * (r + width)].bitcast(FP4X4),
-                    rhs_scale=xs[:, g, n0 : n0 + width],
+                    rhs=x_codes[h][:, g, :].bitcast(FP4X4),
+                    rhs_scale=xs[:, g, 512 * h : 512 * h + 512],
                     start=(g == 0),
                     stop=(g == 1),
                 )
-            nc.scalar.activation(out=th[s, h][:, t, r : r + width], in_=bank[:], func=TANH)
+            nc.scalar.activation(out=th[s, h][:, t, :], in_=bank[:], func=TANH)
 
-        def cols(nh, part):
-            return slice(0, 512) if part is None else slice(256 * part, 256 * part + 256)
-
-        def interleave_w(k, nh, part=None, eng="v"):
-            c = cols(nh, part)
-            dst = w_il[k, nh][:].rearrange("p (n t) -> p n t", t=4)[:, c, :]
-            src = w_raw[k, nh][:, :, c].rearrange("p t n -> p n t")
-            if eng == "v":
-                nc.vector.tensor_copy(out=dst, in_=src)
-            else:
-                nc.scalar.copy(out=dst, in_=src)
-
-        def negate_b(nh, part=None):
-            c = cols(nh, part)
-            c4 = slice(4 * c.start, 4 * c.stop)
-            nc.vector.tensor_scalar(
-                out=w_il["nb", nh][:, c4], in0=w_il["b", nh][:, c4], scalar1=-1.0, scalar2=None, op0=MULT
-            )
-
-        def quant_w(k, nh, part=None):
-            c = cols(nh, part)
-            nc.vector.quantize_mx(
-                out=w_codes[k, nh][:, c].bitcast(FP8X4),
-                scales=w_sc[k, nh][:, c],
-                in_=w_il[k, nh][:, 4 * c.start : 4 * c.stop],
-            )
-
-        def mul_gain(s, n0, width):
-            h, r = n0 // 512, n0 % 512
-            for t in range(4):
-                nc.vector.tensor_scalar(
-                    out=ub[s, h][:, t, r : r + width],
-                    in0=th[s, h][:, t, r : r + width],
-                    scalar1=g_sb[:, 4 * s + t : 4 * s + t + 1],
-                    scalar2=None,
-                    op0=MULT,
-                )
-
-        def interleave_uv(s, m):
-            h, r = m // 4, 128 * (m % 4)
+        def interleave_w(k, nh):
             nc.vector.tensor_copy(
-                out=uv_il[s, m][:].rearrange("p (n t) -> p n t", t=4),
-                in_=ub[s, h][:, :, r : r + 128].rearrange("p t n -> p n t"),
+                out=w_il[k][:, 2048 * nh : 2048 * nh + 2048].rearrange("p (c i t) -> p c t i", i=4, t=4),
+                in_=w_raw[k][:, :, 512 * nh : 512 * nh + 512].rearrange("p t (c i) -> p c t i", i=4),
+            )
+
+        def quant_w(k, nh):
+            n = slice(512 * nh, 512 * nh + 512)
+            nc.vector.quantize_mx(
+                out=w_codes[k][:, n].bitcast(FP8X4),
+                scales=w_sc[k][:, n],
+                in_=w_il[k][:, 2048 * nh : 2048 * nh + 2048],
+            )
+
+        def mul_gain(s, m):
+            h, r = m // 4, 128 * (m % 4)
+            nc.vector.tensor_tensor(
+                out=uv_il[s, m][:].rearrange("p (c i t) -> p c t i", i=2, t=4),
+                in0=th[s, h][:, :, r : r + 128].rearrange("p t (c i) -> p c t i", i=2),
+                in1=g_sb[:, s, :, :].unsqueeze(1).to_broadcast([128, 64, 4, 2]),
+                op=MULT,
             )
 
         def quant_uv(s, m):
             nc.vector.quantize_mx(out=uv_codes[s, m][:].bitcast(FP8X4), scales=uv_sc[s, m][:], in_=uv_il[s, m][:])
 
-        def mm2(bank, s, m, k, nh, start, stop, part=None):
-            c = cols(nh, part)
-            nc.tensor.matmul_mx(
-                out=bank,
-                lhsT=uv_codes[s, m][:].bitcast(FP8X4),
-                lhsT_scale=uv_sc[s, m][:],
-                rhs=w_codes[k, nh][:, c].bitcast(FP8X4),
-                rhs_scale=w_sc[k, nh][:, c],
-                start=start,
-                stop=stop,
-            )
+        y = {}
 
-        def group(m, nh, ri, y, ycol, eng):
+        def group(m, ri, nh, eng):
             bank = psum.tile([128, 512], F32, name="bank")
-            ks = ("c", "nb") if ri == 0 else ("b", "c")
-            mm2(bank[:], 0, m, ks[0], nh, True, False)
-            mm2(bank[:], 1, m, ks[1], nh, False, True)
+            for s in range(2):
+                k = (("c", "nb"), ("b", "c"))[ri][s]
+                n = slice(512 * nh, 512 * nh + 512)
+                nc.tensor.matmul_mx(
+                    out=bank[:],
+                    lhsT=uv_codes[s, m][:].bitcast(FP8X4),
+                    lhsT_scale=uv_sc[s, m][:],
+                    rhs=w_codes[k][:, n].bitcast(FP8X4),
+                    rhs_scale=w_sc[k][:, n],
+                    start=(s == 0),
+                    stop=(s == 1),
+                )
+            if nh == 0:
+                y[m, ri] = ypool.tile([128, 1024], F32, name="y")
+            dst = y[m, ri][:, 512 * nh : 512 * nh + 512]
             if eng == "s":
-                nc.scalar.copy(out=y[:, ycol : ycol + 512], in_=bank[:])
+                nc.scalar.copy(out=dst, in_=bank[:])
             else:
-                nc.vector.tensor_copy(out=y[:, ycol : ycol + 512], in_=bank[:])
+                nc.vector.tensor_copy(out=dst, in_=bank[:])
 
-        def store(m, ri, y, n0, width):
+        def store(m, ri, n=slice(0, 1024)):
             out = (out_0, out_1)[ri]
-            nc.sync.dma_start(out=out[m * 128 : (m + 1) * 128, n0 : n0 + width], in_=y[:])
+            nc.sync.dma_start(out=out[128 * m : 128 * m + 128, n], in_=y[m, ri][:, n])
 
-        def half_rows(m, nh, ri, eng):
-            y = ypool.tile([128, 512], F32, name="yh")
-            group(m, nh, ri, y, 0, eng)
-            store(m, ri, y, nh * 512, 512)
+        def rows(m, ri, engs="ss"):
+            for nh in range(2):
+                group(m, ri, nh, engs[nh])
+            store(m, ri)
 
-        def full_rows(m, ri, engs):
-            y = yfull.tile([128, 1024], F32, name="yf")
-            group(m, 0, ri, y, 0, engs[0])
-            group(m, 1, ri, y, 512, engs[1])
-            store(m, ri, y, 0, 1024)
-
-        def quarter(m, part, y):
-            bank = psum.tile([128, 2, 256], F32, name="bank")
-            for ri, ks in ((1, ("b", "c")), (0, ("c", "nb"))):
-                for s in range(2):
-                    mm2(bank[:, ri, :], s, m, ks[s], 1, s == 0, s == 1, part)
-            nc.scalar.copy(out=y[:, :, 256 * part : 256 * part + 256], in_=bank[:])
+        def negate_b(nh):
+            n = slice(2048 * nh, 2048 * nh + 2048)
+            nc.vector.tensor_scalar(out=w_il["nb"][:, n], in0=w_il["b"][:, n], scalar1=-1.0, scalar2=None, op0=MULT)
 
         def samples(m):
-            interleave_uv(0, m)
-            interleave_uv(1, m)
+            mul_gain(0, m)
+            mul_gain(1, m)
             quant_uv(0, m)
             quant_uv(1, m)
 
-        for n0 in (0, 256):
-            for s in range(2):
-                for t in range(4):
-                    stage1(s, t, n0, 256)
-            if n0 == 0:
-                g_ps = psum.tile([128, 128], BF16, name="bank")
-                nc.tensor.transpose(g_ps[:], g_rows[:], ident[:])
-        interleave_w("c", 1, None, "s")
-        stage1(0, 0, 512, 512)
-        stage1(0, 1, 512, 512)
+        def half(m, ri, nh, eng="s"):
+            group(m, ri, nh, eng)
+            store(m, ri, slice(512 * nh, 512 * nh + 512))
 
-        interleave_w("c", 0)
-        interleave_w("b", 0)
-        quant_w("c", 0)
-        nc.vector.tensor_copy(out=g_sb[:], in_=g_ps[:, 0:8])
-        quant_w("b", 0)
-        mul_gain(0, 0, 256)
-        mul_gain(1, 0, 256)
-        samples(0)
-        half_rows(0, 0, 1, "s")
+        for s in range(2):
+            for t in range(4):
+                stage1(s, t, 0)
+        g_ps = psum.tile([128, 2, 128], BF16, name="bank")
+        for s in range(2):
+            nc.tensor.transpose(g_ps[:, s, :], g_rows[:, s, :], ident[:])
+        for s in range(2):
+            for t in range(4):
+                stage1(s, t, 1)
+        for k in ("c", "b"):
+            interleave_w(k, 0)
+            interleave_w(k, 1)
+            quant_w(k, 0)
+            if k == "b":
+                nc.vector.tensor_copy(out=g_sb[:], in_=g_ps[:, :, 0:4].unsqueeze(3).to_broadcast([128, 2, 4, 2]))
+                samples(0)
+            quant_w(k, 1)
+        half(0, 1, 0)
+        half(0, 1, 1)
         negate_b(0)
-        mul_gain(0, 256, 256)
+        mul_gain(0, 1)
         quant_w("nb", 0)
-        half_rows(0, 0, 0, "s")
-        for t in (2, 3):
-            stage1(0, t, 512, 512)
-        for t in (0, 1):
-            stage1(1, t, 512, 512)
-        interleave_w("b", 1)
-        quant_w("c", 1)
-        quant_w("b", 1)
-        negate_b(1)
-        interleave_uv(0, 1)
-        quant_w("nb", 1)
-        half_rows(0, 1, 1, "s")
-        half_rows(0, 1, 0, "s")
-        interleave_uv(1, 1)
+        half(0, 0, 0)
+        mul_gain(1, 1)
         quant_uv(0, 1)
         quant_uv(1, 1)
-        mul_gain(1, 256, 256)
-        full_rows(1, 1, "ss")
-        full_rows(1, 0, "ss")
-        for t in (2, 3):
-            stage1(1, t, 512, 512)
-        samples(2)
-        samples(3)
-        mul_gain(0, 512, 512)
-        mul_gain(1, 512, 512)
-        for m in range(4, 8):
+        rows(1, 1)
+        group(1, 0, 0, "s")
+        negate_b(1)
+        mul_gain(0, 2)
+        quant_w("nb", 1)
+        half(0, 0, 1)
+        group(1, 0, 1, "s")
+        store(1, 0)
+        mul_gain(1, 2)
+        quant_uv(0, 2)
+        quant_uv(1, 2)
+        for m in range(3, 8):
             samples(m)
         for m in range(2, 8):
             for ri in (1, 0):
-                if m < 7 or ri > 0:
-                    full_rows(m, ri, "ss" if m < 5 else "vs")
+                engs = "ss" if m < VFROM else "vs"
+                if (m, ri) != (7, 0):
+                    rows(m, ri, engs)
                 else:
-                    half_rows(m, 0, ri, "v")
-                    half_rows(m, 1, ri, "s")
+                    for nh in range(2):
+                        group(m, ri, nh, engs[nh])
+                        store(m, ri, slice(512 * nh, 512 * nh + 512))

@@ -3,7 +3,8 @@ from contextlib import ExitStack
 import concourse.mybir as mybir
 from concourse.masks import make_identity
 
-FLOPS = 2 * 1024 * 1024 * 1024 + 4 * 2 * 1024 * 512 * 1024
+SAMPLES, STREAMS, CHAINS, ANTENNAS = 1024, 1024, 512, 1024
+FLOPS = 2 * SAMPLES * STREAMS * 2 * CHAINS + 4 * 2 * SAMPLES * CHAINS * ANTENNAS
 
 F32 = mybir.dt.float32
 BF16 = mybir.dt.bfloat16
@@ -14,8 +15,16 @@ FP4X4 = mybir.dt.float4_e2m1fn_x4
 FP8X4 = mybir.dt.float8_e4m3fn_x4
 TANH = mybir.ActivationFunctionType.Tanh
 MULT = mybir.AluOpType.mult
-WARM = 8
-VFROM = 5
+
+P = 128
+SLOTS = 4
+GROUPS = STREAMS // 512
+HALF = 512
+PHASES = 2
+U, V = 0, 1
+RE, IM = 0, 1
+BLOCKS = SAMPLES // P
+WARM_UP = 10
 
 
 def tile_hybrid_beamforming_precoder_s4_kernel(
@@ -24,237 +33,245 @@ def tile_hybrid_beamforming_precoder_s4_kernel(
     nc = tc.nc
     with ExitStack() as ctx:
         keep = ctx.enter_context(tc.tile_pool(name="keep", bufs=1))
-        ypool = ctx.enter_context(tc.tile_pool(name="ypool", bufs=16))
+        rows_pool = ctx.enter_context(tc.tile_pool(name="rows", bufs=PHASES * BLOCKS))
         psum = ctx.enter_context(tc.psum_pool(name="psum", bufs=8))
 
-        def kt(shape, dtype, name):
+        def tile(shape, dtype, name):
             return keep.tile(shape, dtype, name=name, align_bytes=64)
 
-        d_raw = kt([128, 2, 2048], U8, "d_raw")
-        d_codes = {s: kt([128, 4, 2, 256], U8, "d_codes%d" % s) for s in range(2)}
-        ds_raw = kt([128, 2, 1024], U8, "ds_raw")
-        ds = kt([128, 4, 2, 2, 128], U8, "ds")
-        x_codes = {h: kt([128, 2, 1024], U8, "x_codes%d" % h) for h in range(2)}
-        xs = kt([128, 2, 1024], U8, "xs")
-        g_rows = kt([128, 2, 128], BF16, "g_rows")
-        ident = kt([128, 128], BF16, "ident")
-        g_sb = kt([128, 2, 4, 2], F32, "g_sb")
-        warm = kt([128, 1], F32, "warm")
+        x_codes = {h: tile([P, GROUPS, 2 * HALF], U8, "x_codes%d" % h) for h in range(2)}
+        x_scales = tile([P, GROUPS, SAMPLES], U8, "x_scales")
+        d_raw = tile([P, GROUPS, 2 * PHASES * CHAINS], U8, "d_raw")
+        d_scales_raw = tile([P, GROUPS, PHASES * CHAINS], U8, "d_scales_raw")
+        d_codes = {s: tile([P, GROUPS, SLOTS, 2 * P], U8, "d_codes%d" % s) for s in (U, V)}
+        d_scales = tile([P, SLOTS, GROUPS, PHASES, P], U8, "d_scales")
+        gain_rows = tile([P, PHASES, P], BF16, "gain_rows")
+        identity = tile([P, P], BF16, "identity")
+        gain_cols = tile([P, PHASES * SLOTS], F32, "gain_cols")
+        dummy = tile([P, 1], F32, "dummy")
 
-        w_raw, w_il, w_codes, w_sc = {}, {}, {}, {}
-        for k in ("c", "b"):
-            w_raw[k] = kt([128, 4, 1024], BF16, "raw_" + k)
-        for k in ("c", "b", "nb"):
-            w_il[k] = kt([128, 4096], BF16, "il_" + k)
-            w_codes[k] = kt([128, 1024], U32, "wq_" + k)
-            w_sc[k] = kt([128, 1024], U8, "ws_" + k)
-        th, uv_il, uv_codes, uv_sc = {}, {}, {}, {}
-        for s in range(2):
-            for h in range(2):
-                th[s, h] = kt([128, 4, 512], F32, "th_%d%d" % (s, h))
-            for m in range(8):
-                uv_il[s, m] = kt([128, 512], BF16, "uvil_%d%d" % (s, m))
-                uv_codes[s, m] = kt([128, 128], U32, "uvq_%d%d" % (s, m))
-                uv_sc[s, m] = kt([128, 128], U8, "uvs_%d%d" % (s, m))
+        w_raw = {(k, nh): tile([P, SLOTS, HALF], BF16, "raw_%s%d" % (k, nh)) for k in ("c", "b") for nh in range(2)}
+        w_packed = {k: tile([P, SLOTS * ANTENNAS], BF16, "packed_" + k) for k in ("c", "b", "nb")}
+        w_codes = {k: tile([P, ANTENNAS], U32, "codes_" + k) for k in ("c", "b", "nb")}
+        w_scales = {k: tile([P, ANTENNAS], U8, "scales_" + k) for k in ("c", "b", "nb")}
+
+        tanh_h = {(s, h): tile([P, SLOTS, HALF], F32, "tanh_%d%d" % (s, h)) for s in (U, V) for h in range(2)}
+        rounded = {(s, q): tile([P, SLOTS, 256], BF16, "rounded_%d%d" % (s, q)) for s in (U, V) for q in range(4)}
+        uv_packed = {(s, m): tile([P, SLOTS * P], BF16, "uv_packed_%d%d" % (s, m)) for s in (U, V) for m in range(BLOCKS)}
+        uv_codes = {(s, m): tile([P, P], U32, "uv_codes_%d%d" % (s, m)) for s in (U, V) for m in range(BLOCKS)}
+        uv_scales = {(s, m): tile([P, P], U8, "uv_scales_%d%d" % (s, m)) for s in (U, V) for m in range(BLOCKS)}
 
         ctx.enter_context(tc.manual_schedule())
 
-        def flat_i32(t, pattern):
+        def words(t, pattern):
             return t[:].rearrange(pattern).bitcast(I32)
 
-        def load_x(eng, h):
-            eng.dma_start(
-                out=x_codes[h][:].bitcast(I32),
-                in_=sym_words.rearrange("g p x -> p g x")[:, :, h * 1024 : (h + 1) * 1024].bitcast(I32),
-            )
-
-        def load_scales(eng, dst, src, quad):
-            eng.dma_start(
-                out=dst[32 * quad : 32 * quad + 4, :, :].bitcast(I32),
-                in_=src[:, 4 * quad : 4 * quad + 4, :].rearrange("g q n -> q g n").bitcast(I32),
-            )
-
-        def load_w(eng, k):
-            w = (cosw if k == "c" else sinw).rearrange("(b t i) n -> i b t n", t=4, i=4)
-            for i in range(4):
-                eng.dma_start(out=w_raw[k][i:128:4, :, :], in_=w[i])
-
-        nc.vector.memset(flat_i32(ds_raw, "p g n -> p (g n)"), 0)
-        nc.vector.memset(flat_i32(xs, "p g n -> p (g n)"), 0)
-        nc.vector.memset(g_rows[:], 0.0)
-        nc.vector.memset(flat_i32(ds, "p t g s n -> p (t g s n)"), 0)
+        nc.vector.memset(words(d_scales_raw, "p g n -> p (g n)"), 0)
+        nc.vector.memset(words(x_scales, "p g n -> p (g n)"), 0)
+        nc.vector.memset(gain_rows[:], 0.0)
+        nc.vector.memset(w_scales["c"][:].bitcast(I32), 0)
         nc.vector.memset(x_codes[1][:, 0, :].bitcast(I32), 0)
-        nc.vector.memset(warm[:], 0.0)
-        ds_flat = ds[:].rearrange("p t g s n -> p (t g s n)")
-        warm_bank = psum.tile([128, 512], F32, name="bank")
-        for k in range(WARM):
+        nc.vector.memset(dummy[:], 0.0)
+
+        warm_bank = psum.tile([P, HALF], F32, name="bank")
+        for unused in range(WARM_UP):
             nc.tensor.matmul_mx(
                 out=warm_bank[:],
-                lhsT=x_codes[1][:, 0, 0:256].bitcast(FP4X4),
-                lhsT_scale=ds_flat[:, 0:128],
+                lhsT=x_codes[1][:, 0, 0 : 2 * P].bitcast(FP4X4),
+                lhsT_scale=w_scales["c"][:, 0:P],
                 rhs=x_codes[1][:, 0, :].bitcast(FP4X4),
-                rhs_scale=ds_flat[:, 512:1024],
+                rhs_scale=w_scales["c"][:, HALF : 2 * HALF],
                 start=True,
                 stop=True,
             )
-        nc.sync.dma_start(out=d_raw[:].bitcast(I32), in_=dig_words.rearrange("g p x -> p g x").bitcast(I32))
-        load_x(nc.sync, 0)
-        for quad in range(4):
-            load_scales(nc.scalar, ds_raw, dig_scales, quad)
-        for quad in range(4):
-            load_scales(nc.scalar if quad < 2 else nc.gpsimd, xs, sym_scales, quad)
+
+        def load_x(engine, h):
+            by_partition = sym_words.rearrange("g p x -> p g x")
+            engine.dma_start(
+                out=x_codes[h][:].bitcast(I32),
+                in_=by_partition[:, :, 2 * HALF * h : 2 * HALF * (h + 1)].bitcast(I32),
+            )
+
+        def load_scales(engine, dst, src):
+            for j in range(4):
+                engine.dma_start(
+                    out=dst[32 * j : 32 * j + 4, :, :].bitcast(I32),
+                    in_=src[:, 4 * j : 4 * j + 4, :].rearrange("g r n -> r g n").bitcast(I32),
+                )
+
+        def load_w(engine, k, nh):
+            w = (cosw if k == "c" else sinw).rearrange("(b t i) n -> t b i n", t=SLOTS, i=4)
+            for t in range(SLOTS):
+                engine.dma_start(out=w_raw[k, nh][:, t, :], in_=w[t][:, :, HALF * nh : HALF * (nh + 1)])
+
+        nc.gpsimd.dma_start(out=d_raw[:].bitcast(I32), in_=dig_words.rearrange("g p x -> p g x").bitcast(I32))
+        load_x(nc.gpsimd, 0)
+        load_scales(nc.scalar, d_scales_raw, dig_scales)
+        load_scales(nc.sync, x_scales, sym_scales)
         nc.gpsimd.dma_start(
-            out=g_rows[0:4, :, :].rearrange("t s (b i) -> t (s b) i", i=4),
-            in_=gain.rearrange("(c t i) -> t c i", t=4, i=4),
+            out=gain_rows[0:SLOTS, :, :].rearrange("t s (b i) -> t (s b) i", i=4),
+            in_=gain.rearrange("(c t i) -> t c i", t=SLOTS, i=4),
         )
-        make_identity(nc, ident[:])
-        nc.scalar.activation(out=warm[:], in_=warm[:], func=TANH)
-        load_w(nc.sync, "c")
-        load_w(nc.sync, "b")
+        make_identity(nc, identity[:])
+        nc.scalar.activation(out=dummy[:], in_=dummy[:], func=TANH)
+        load_w(nc.sync, "c", 0)
+        load_w(nc.sync, "b", 0)
         load_x(nc.sync, 1)
+        load_w(nc.sync, "c", 1)
+        load_w(nc.sync, "b", 1)
 
         nc.vector.tensor_copy(
-            out=flat_i32(ds, "p t g s n -> p (t g s n)").rearrange("p (t c) -> p t c", t=4),
-            in_=flat_i32(ds_raw, "p g n -> p (g n)").rearrange("p (c t) -> p t c", t=4),
+            out=words(d_scales, "p t g s n -> p (t g s n)").rearrange("p (t c) -> p t c", t=SLOTS),
+            in_=words(d_scales_raw, "p g n -> p (g n)").rearrange("p (c t) -> p t c", t=SLOTS),
         )
-        d_src = flat_i32(d_raw, "p g x -> p (g x)").rearrange("p (g s c t w) -> p g s t c w", g=2, s=2, t=4, w=2)
-        for s in range(2):
-            d_dst = flat_i32(d_codes[s], "p t g n -> p (t g n)").rearrange("p (t g c w) -> p g t c w", t=4, g=2, w=2)
-            for g in range(2):
+        d_src = words(d_raw, "p g x -> p (g x)").rearrange("p (g s c t w) -> p g s t c w", g=GROUPS, s=PHASES, t=SLOTS, w=2)
+        for s in (U, V):
+            d_dst = words(d_codes[s], "p g t n -> p (g t n)").rearrange("p (g t c w) -> p g t c w", g=GROUPS, t=SLOTS, w=2)
+            for g in range(GROUPS):
                 nc.vector.tensor_copy(out=d_dst[:, g], in_=d_src[:, g, s])
 
-        def stage1(s, t, h):
-            bank = psum.tile([128, 512], F32, name="bank")
-            for g in range(2):
+        def chains(s, t, h):
+            bank = psum.tile([P, HALF], F32, name="bank")
+            for g in range(GROUPS):
                 nc.tensor.matmul_mx(
                     out=bank[:],
-                    lhsT=d_codes[s][:, t, g, :].bitcast(FP4X4),
-                    lhsT_scale=ds[:, t, g, s, :],
+                    lhsT=d_codes[s][:, g, t, :].bitcast(FP4X4),
+                    lhsT_scale=d_scales[:, t, g, s, :],
                     rhs=x_codes[h][:, g, :].bitcast(FP4X4),
-                    rhs_scale=xs[:, g, 512 * h : 512 * h + 512],
+                    rhs_scale=x_scales[:, g, HALF * h : HALF * (h + 1)],
                     start=(g == 0),
-                    stop=(g == 1),
+                    stop=(g == GROUPS - 1),
                 )
-            nc.scalar.activation(out=th[s, h][:, t, :], in_=bank[:], func=TANH)
+            nc.scalar.activation(out=tanh_h[s, h][:, t, :], in_=bank[:], func=TANH)
 
-        def interleave_w(k, nh):
+        def packed_half(k, nh):
+            return w_packed[k][:, SLOTS * HALF * nh : SLOTS * HALF * (nh + 1)]
+
+        def pack_w(copy, k, nh):
+            copy(
+                out=packed_half(k, nh).rearrange("p (n t) -> p n t", t=SLOTS),
+                in_=w_raw[k, nh][:].rearrange("p t n -> p n t"),
+            )
+
+        def negate_b(nh):
+            nc.vector.tensor_scalar(out=packed_half("nb", nh), in0=packed_half("b", nh), scalar1=-1.0, scalar2=None, op0=MULT)
+
+        def quantise_w(k, nh):
+            n = slice(HALF * nh, HALF * (nh + 1))
+            nc.vector.quantize_mx(out=w_codes[k][:, n].bitcast(FP8X4), scales=w_scales[k][:, n], in_=packed_half(k, nh))
+
+        def times_gain(s, q):
+            n = 256 * (q % 2)
+            for t in range(SLOTS):
+                nc.vector.tensor_scalar(
+                    out=rounded[s, q][:, t, :],
+                    in0=tanh_h[s, q // 2][:, t, n : n + 256],
+                    scalar1=gain_cols[:, SLOTS * s + t : SLOTS * s + t + 1],
+                    scalar2=None,
+                    op0=MULT,
+                )
+
+        def pack_uv(s, m):
+            n = P * (m % 2)
             nc.vector.tensor_copy(
-                out=w_il[k][:, 2048 * nh : 2048 * nh + 2048].rearrange("p (c i t) -> p c t i", i=4, t=4),
-                in_=w_raw[k][:, :, 512 * nh : 512 * nh + 512].rearrange("p t (c i) -> p c t i", i=4),
+                out=uv_packed[s, m][:].rearrange("p (n t) -> p n t", t=SLOTS),
+                in_=rounded[s, m // 2][:, :, n : n + P].rearrange("p t n -> p n t"),
             )
 
-        def quant_w(k, nh):
-            n = slice(512 * nh, 512 * nh + 512)
-            nc.vector.quantize_mx(
-                out=w_codes[k][:, n].bitcast(FP8X4),
-                scales=w_sc[k][:, n],
-                in_=w_il[k][:, 2048 * nh : 2048 * nh + 2048],
-            )
+        def quantise_uv(s, m):
+            nc.vector.quantize_mx(out=uv_codes[s, m][:].bitcast(FP8X4), scales=uv_scales[s, m][:], in_=uv_packed[s, m][:])
 
-        def mul_gain(s, m):
-            h, r = m // 4, 128 * (m % 4)
-            nc.vector.tensor_tensor(
-                out=uv_il[s, m][:].rearrange("p (c i t) -> p c t i", i=2, t=4),
-                in0=th[s, h][:, :, r : r + 128].rearrange("p t (c i) -> p c t i", i=2),
-                in1=g_sb[:, s, :, :].unsqueeze(1).to_broadcast([128, 64, 4, 2]),
-                op=MULT,
-            )
+        def block(m):
+            if m % 2 == 0:
+                times_gain(U, m // 2)
+                times_gain(V, m // 2)
+            pack_uv(U, m)
+            pack_uv(V, m)
+            quantise_uv(U, m)
+            quantise_uv(V, m)
 
-        def quant_uv(s, m):
-            nc.vector.quantize_mx(out=uv_codes[s, m][:].bitcast(FP8X4), scales=uv_sc[s, m][:], in_=uv_il[s, m][:])
+        row_tiles = {}
 
-        y = {}
-
-        def group(m, ri, nh, eng):
-            bank = psum.tile([128, 512], F32, name="bank")
-            for s in range(2):
-                k = (("c", "nb"), ("b", "c"))[ri][s]
-                n = slice(512 * nh, 512 * nh + 512)
+        def product(m, part, nh, copy):
+            bank = psum.tile([P, HALF], F32, name="bank")
+            n = slice(HALF * nh, HALF * (nh + 1))
+            for s in (U, V):
+                k = (("c", "nb"), ("b", "c"))[part][s]
                 nc.tensor.matmul_mx(
                     out=bank[:],
                     lhsT=uv_codes[s, m][:].bitcast(FP8X4),
-                    lhsT_scale=uv_sc[s, m][:],
+                    lhsT_scale=uv_scales[s, m][:],
                     rhs=w_codes[k][:, n].bitcast(FP8X4),
-                    rhs_scale=w_sc[k][:, n],
-                    start=(s == 0),
-                    stop=(s == 1),
+                    rhs_scale=w_scales[k][:, n],
+                    start=(s == U),
+                    stop=(s == V),
                 )
             if nh == 0:
-                y[m, ri] = ypool.tile([128, 1024], F32, name="y")
-            dst = y[m, ri][:, 512 * nh : 512 * nh + 512]
-            if eng == "s":
-                nc.scalar.copy(out=dst, in_=bank[:])
-            else:
-                nc.vector.tensor_copy(out=dst, in_=bank[:])
+                row_tiles[m, part] = rows_pool.tile([P, ANTENNAS], F32, name="row")
+            copy(out=row_tiles[m, part][:, n], in_=bank[:])
 
-        def store(m, ri, n=slice(0, 1024)):
-            out = (out_0, out_1)[ri]
-            nc.sync.dma_start(out=out[128 * m : 128 * m + 128, n], in_=y[m, ri][:, n])
+        def store(m, part, first, last):
+            out = (out_0, out_1)[part]
+            nc.sync.dma_start(out=out[P * m : P * (m + 1), first:last], in_=row_tiles[m, part][:, first:last])
 
-        def rows(m, ri, engs="ss"):
-            for nh in range(2):
-                group(m, ri, nh, engs[nh])
-            store(m, ri)
+        def half_rows(m, part, nh, copy=nc.scalar.copy):
+            product(m, part, nh, copy)
+            store(m, part, HALF * nh, HALF * (nh + 1))
 
-        def negate_b(nh):
-            n = slice(2048 * nh, 2048 * nh + 2048)
-            nc.vector.tensor_scalar(out=w_il["nb"][:, n], in0=w_il["b"][:, n], scalar1=-1.0, scalar2=None, op0=MULT)
+        for s in (U, V):
+            for t in range(SLOTS):
+                chains(s, t, 0)
+        gain_bank = psum.tile([P, PHASES, P], BF16, name="bank")
+        for s in (U, V):
+            nc.tensor.transpose(gain_bank[:, s, :], gain_rows[:, s, :], identity[:])
+        pack_w(nc.scalar.copy, "c", 1)
+        for t in range(SLOTS):
+            chains(U, t, 1)
 
-        def samples(m):
-            mul_gain(0, m)
-            mul_gain(1, m)
-            quant_uv(0, m)
-            quant_uv(1, m)
-
-        def half(m, ri, nh, eng="s"):
-            group(m, ri, nh, eng)
-            store(m, ri, slice(512 * nh, 512 * nh + 512))
-
-        for s in range(2):
-            for t in range(4):
-                stage1(s, t, 0)
-        g_ps = psum.tile([128, 2, 128], BF16, name="bank")
-        for s in range(2):
-            nc.tensor.transpose(g_ps[:, s, :], g_rows[:, s, :], ident[:])
-        for s in range(2):
-            for t in range(4):
-                stage1(s, t, 1)
-        for k in ("c", "b"):
-            interleave_w(k, 0)
-            interleave_w(k, 1)
-            quant_w(k, 0)
-            if k == "b":
-                nc.vector.tensor_copy(out=g_sb[:], in_=g_ps[:, :, 0:4].unsqueeze(3).to_broadcast([128, 2, 4, 2]))
-                samples(0)
-            quant_w(k, 1)
-        half(0, 1, 0)
-        half(0, 1, 1)
+        pack_w(nc.vector.tensor_copy, "c", 0)
+        pack_w(nc.vector.tensor_copy, "b", 0)
+        quantise_w("c", 0)
+        nc.vector.tensor_copy(out=gain_cols[:].rearrange("p (s t) -> p s t", s=PHASES), in_=gain_bank[:, :, 0:SLOTS])
+        quantise_w("b", 0)
+        block(0)
+        half_rows(0, IM, 0)
         negate_b(0)
-        mul_gain(0, 1)
-        quant_w("nb", 0)
-        half(0, 0, 0)
-        mul_gain(1, 1)
-        quant_uv(0, 1)
-        quant_uv(1, 1)
-        rows(1, 1)
-        group(1, 0, 0, "s")
+        pack_uv(U, 1)
+        quantise_w("nb", 0)
+        half_rows(0, RE, 0)
+        pack_uv(V, 1)
+        quantise_uv(U, 1)
+        quantise_uv(V, 1)
+        half_rows(1, IM, 0)
+        half_rows(1, RE, 0)
+        for t in range(SLOTS):
+            chains(V, t, 1)
+
+        pack_w(nc.vector.tensor_copy, "b", 1)
+        quantise_w("c", 1)
+        quantise_w("b", 1)
+        for m in (0, 1):
+            half_rows(m, IM, 1)
         negate_b(1)
-        mul_gain(0, 2)
-        quant_w("nb", 1)
-        half(0, 0, 1)
-        group(1, 0, 1, "s")
-        store(1, 0)
-        mul_gain(1, 2)
-        quant_uv(0, 2)
-        quant_uv(1, 2)
-        for m in range(3, 8):
-            samples(m)
-        for m in range(2, 8):
-            for ri in (1, 0):
-                engs = "ss" if m < VFROM else "vs"
-                if (m, ri) != (7, 0):
-                    rows(m, ri, engs)
+        times_gain(U, 1)
+        quantise_w("nb", 1)
+        for m in (0, 1):
+            half_rows(m, RE, 1)
+        times_gain(V, 1)
+        pack_uv(U, 2)
+        pack_uv(V, 2)
+        quantise_uv(U, 2)
+        quantise_uv(V, 2)
+        for m in range(3, BLOCKS):
+            block(m)
+
+        for m in range(2, BLOCKS):
+            first_copy = nc.scalar.copy if m < 6 else nc.vector.tensor_copy
+            for part in (IM, RE):
+                if (m, part) == (BLOCKS - 1, RE):
+                    half_rows(m, part, 0, first_copy)
+                    half_rows(m, part, 1)
                 else:
-                    for nh in range(2):
-                        group(m, ri, nh, engs[nh])
-                        store(m, ri, slice(512 * nh, 512 * nh + 512))
+                    product(m, part, 0, first_copy)
+                    product(m, part, 1, nc.scalar.copy)
+                    store(m, part, 0, ANTENNAS)

from contextlib import ExitStack

import concourse.mybir as mybir
from concourse.masks import make_identity

SAMPLES, STREAMS, CHAINS, ANTENNAS = 1024, 1024, 512, 1024
FLOPS = 2 * SAMPLES * STREAMS * 2 * CHAINS + 4 * 2 * SAMPLES * CHAINS * ANTENNAS

F32 = mybir.dt.float32
BF16 = mybir.dt.bfloat16
I32 = mybir.dt.int32
U32 = mybir.dt.uint32
U8 = mybir.dt.uint8
FP4X4 = mybir.dt.float4_e2m1fn_x4
FP8X4 = mybir.dt.float8_e4m3fn_x4
TANH = mybir.ActivationFunctionType.Tanh
MULT = mybir.AluOpType.mult

P = 128
SLOTS = 4
GROUPS = STREAMS // 512
HALF = 512
PHASES = 2
U, V = 0, 1
RE, IM = 0, 1
BLOCKS = SAMPLES // P
WARM_UP = 10


def tile_hybrid_beamforming_precoder_s4_kernel(
    tc, sym_words, sym_scales, dig_words, dig_scales, gain, cosw, sinw, out_0, out_1
):
    nc = tc.nc
    with ExitStack() as ctx:
        keep = ctx.enter_context(tc.tile_pool(name="keep", bufs=1))
        rows_pool = ctx.enter_context(tc.tile_pool(name="rows", bufs=PHASES * BLOCKS))
        psum = ctx.enter_context(tc.psum_pool(name="psum", bufs=8))

        def tile(shape, dtype, name):
            return keep.tile(shape, dtype, name=name, align_bytes=64)

        x_codes = {h: tile([P, GROUPS, 2 * HALF], U8, "x_codes%d" % h) for h in range(2)}
        x_scales = tile([P, GROUPS, SAMPLES], U8, "x_scales")
        d_raw = tile([P, GROUPS, 2 * PHASES * CHAINS], U8, "d_raw")
        d_scales_raw = tile([P, GROUPS, PHASES * CHAINS], U8, "d_scales_raw")
        d_codes = {s: tile([P, GROUPS, SLOTS, 2 * P], U8, "d_codes%d" % s) for s in (U, V)}
        d_scales = tile([P, SLOTS, GROUPS, PHASES, P], U8, "d_scales")
        gain_rows = tile([P, PHASES, P], BF16, "gain_rows")
        identity = tile([P, P], BF16, "identity")
        gain_cols = tile([P, PHASES * SLOTS], F32, "gain_cols")
        dummy = tile([P, 1], F32, "dummy")

        w_raw = {(k, nh): tile([P, SLOTS, HALF], BF16, "raw_%s%d" % (k, nh)) for k in ("c", "b") for nh in range(2)}
        w_packed = {k: tile([P, SLOTS * ANTENNAS], BF16, "packed_" + k) for k in ("c", "b", "nb")}
        w_codes = {k: tile([P, ANTENNAS], U32, "codes_" + k) for k in ("c", "b", "nb")}
        w_scales = {k: tile([P, ANTENNAS], U8, "scales_" + k) for k in ("c", "b", "nb")}

        tanh_h = {(s, h): tile([P, SLOTS, HALF], F32, "tanh_%d%d" % (s, h)) for s in (U, V) for h in range(2)}
        rounded = {(s, q): tile([P, SLOTS, 256], BF16, "rounded_%d%d" % (s, q)) for s in (U, V) for q in range(4)}
        uv_packed = {(s, m): tile([P, SLOTS * P], BF16, "uv_packed_%d%d" % (s, m)) for s in (U, V) for m in range(BLOCKS)}
        uv_codes = {(s, m): tile([P, P], U32, "uv_codes_%d%d" % (s, m)) for s in (U, V) for m in range(BLOCKS)}
        uv_scales = {(s, m): tile([P, P], U8, "uv_scales_%d%d" % (s, m)) for s in (U, V) for m in range(BLOCKS)}

        ctx.enter_context(tc.manual_schedule())

        def words(t, pattern):
            return t[:].rearrange(pattern).bitcast(I32)

        nc.vector.memset(words(d_scales_raw, "p g n -> p (g n)"), 0)
        nc.vector.memset(words(x_scales, "p g n -> p (g n)"), 0)
        nc.vector.memset(gain_rows[:], 0.0)
        nc.vector.memset(w_scales["c"][:].bitcast(I32), 0)
        nc.vector.memset(x_codes[1][:, 0, :].bitcast(I32), 0)
        nc.vector.memset(dummy[:], 0.0)

        warm_bank = psum.tile([P, HALF], F32, name="bank")
        for unused in range(WARM_UP):
            nc.tensor.matmul_mx(
                out=warm_bank[:],
                lhsT=x_codes[1][:, 0, 0 : 2 * P].bitcast(FP4X4),
                lhsT_scale=w_scales["c"][:, 0:P],
                rhs=x_codes[1][:, 0, :].bitcast(FP4X4),
                rhs_scale=w_scales["c"][:, HALF : 2 * HALF],
                start=True,
                stop=True,
            )

        def load_x(engine, h):
            by_partition = sym_words.rearrange("g p x -> p g x")
            engine.dma_start(
                out=x_codes[h][:].bitcast(I32),
                in_=by_partition[:, :, 2 * HALF * h : 2 * HALF * (h + 1)].bitcast(I32),
            )

        def load_scales(engine, dst, src):
            for j in range(4):
                engine.dma_start(
                    out=dst[32 * j : 32 * j + 4, :, :].bitcast(I32),
                    in_=src[:, 4 * j : 4 * j + 4, :].rearrange("g r n -> r g n").bitcast(I32),
                )

        def load_w(engine, k, nh):
            w = (cosw if k == "c" else sinw).rearrange("(b t i) n -> t b i n", t=SLOTS, i=4)
            for t in range(SLOTS):
                engine.dma_start(out=w_raw[k, nh][:, t, :], in_=w[t][:, :, HALF * nh : HALF * (nh + 1)])

        nc.gpsimd.dma_start(out=d_raw[:].bitcast(I32), in_=dig_words.rearrange("g p x -> p g x").bitcast(I32))
        load_x(nc.gpsimd, 0)
        load_scales(nc.scalar, d_scales_raw, dig_scales)
        load_scales(nc.sync, x_scales, sym_scales)
        nc.gpsimd.dma_start(
            out=gain_rows[0:SLOTS, :, :].rearrange("t s (b i) -> t (s b) i", i=4),
            in_=gain.rearrange("(c t i) -> t c i", t=SLOTS, i=4),
        )
        make_identity(nc, identity[:])
        nc.scalar.activation(out=dummy[:], in_=dummy[:], func=TANH)
        load_w(nc.sync, "c", 0)
        load_w(nc.sync, "b", 0)
        load_x(nc.sync, 1)
        load_w(nc.sync, "c", 1)
        load_w(nc.sync, "b", 1)

        nc.vector.tensor_copy(
            out=words(d_scales, "p t g s n -> p (t g s n)").rearrange("p (t c) -> p t c", t=SLOTS),
            in_=words(d_scales_raw, "p g n -> p (g n)").rearrange("p (c t) -> p t c", t=SLOTS),
        )
        d_src = words(d_raw, "p g x -> p (g x)").rearrange("p (g s c t w) -> p g s t c w", g=GROUPS, s=PHASES, t=SLOTS, w=2)
        for s in (U, V):
            d_dst = words(d_codes[s], "p g t n -> p (g t n)").rearrange("p (g t c w) -> p g t c w", g=GROUPS, t=SLOTS, w=2)
            for g in range(GROUPS):
                nc.vector.tensor_copy(out=d_dst[:, g], in_=d_src[:, g, s])

        def chains(s, t, h):
            bank = psum.tile([P, HALF], F32, name="bank")
            for g in range(GROUPS):
                nc.tensor.matmul_mx(
                    out=bank[:],
                    lhsT=d_codes[s][:, g, t, :].bitcast(FP4X4),
                    lhsT_scale=d_scales[:, t, g, s, :],
                    rhs=x_codes[h][:, g, :].bitcast(FP4X4),
                    rhs_scale=x_scales[:, g, HALF * h : HALF * (h + 1)],
                    start=(g == 0),
                    stop=(g == GROUPS - 1),
                )
            nc.scalar.activation(out=tanh_h[s, h][:, t, :], in_=bank[:], func=TANH)

        def packed_half(k, nh):
            return w_packed[k][:, SLOTS * HALF * nh : SLOTS * HALF * (nh + 1)]

        def pack_w(copy, k, nh):
            copy(
                out=packed_half(k, nh).rearrange("p (n t) -> p n t", t=SLOTS),
                in_=w_raw[k, nh][:].rearrange("p t n -> p n t"),
            )

        def negate_b(nh):
            nc.vector.tensor_scalar(out=packed_half("nb", nh), in0=packed_half("b", nh), scalar1=-1.0, scalar2=None, op0=MULT)

        def quantise_w(k, nh):
            n = slice(HALF * nh, HALF * (nh + 1))
            nc.vector.quantize_mx(out=w_codes[k][:, n].bitcast(FP8X4), scales=w_scales[k][:, n], in_=packed_half(k, nh))

        def times_gain(s, q):
            n = 256 * (q % 2)
            for t in range(SLOTS):
                nc.vector.tensor_scalar(
                    out=rounded[s, q][:, t, :],
                    in0=tanh_h[s, q // 2][:, t, n : n + 256],
                    scalar1=gain_cols[:, SLOTS * s + t : SLOTS * s + t + 1],
                    scalar2=None,
                    op0=MULT,
                )

        def pack_uv(s, m):
            n = P * (m % 2)
            nc.vector.tensor_copy(
                out=uv_packed[s, m][:].rearrange("p (n t) -> p n t", t=SLOTS),
                in_=rounded[s, m // 2][:, :, n : n + P].rearrange("p t n -> p n t"),
            )

        def quantise_uv(s, m):
            nc.vector.quantize_mx(out=uv_codes[s, m][:].bitcast(FP8X4), scales=uv_scales[s, m][:], in_=uv_packed[s, m][:])

        def block(m):
            if m % 2 == 0:
                times_gain(U, m // 2)
                times_gain(V, m // 2)
            pack_uv(U, m)
            pack_uv(V, m)
            quantise_uv(U, m)
            quantise_uv(V, m)

        row_tiles = {}

        def product(m, part, nh, copy):
            bank = psum.tile([P, HALF], F32, name="bank")
            n = slice(HALF * nh, HALF * (nh + 1))
            for s in (U, V):
                k = (("c", "nb"), ("b", "c"))[part][s]
                nc.tensor.matmul_mx(
                    out=bank[:],
                    lhsT=uv_codes[s, m][:].bitcast(FP8X4),
                    lhsT_scale=uv_scales[s, m][:],
                    rhs=w_codes[k][:, n].bitcast(FP8X4),
                    rhs_scale=w_scales[k][:, n],
                    start=(s == U),
                    stop=(s == V),
                )
            if nh == 0:
                row_tiles[m, part] = rows_pool.tile([P, ANTENNAS], F32, name="row")
            copy(out=row_tiles[m, part][:, n], in_=bank[:])

        def store(m, part, first, last):
            out = (out_0, out_1)[part]
            nc.sync.dma_start(out=out[P * m : P * (m + 1), first:last], in_=row_tiles[m, part][:, first:last])

        def half_rows(m, part, nh, copy=nc.scalar.copy):
            product(m, part, nh, copy)
            store(m, part, HALF * nh, HALF * (nh + 1))

        for s in (U, V):
            for t in range(SLOTS):
                chains(s, t, 0)
        gain_bank = psum.tile([P, PHASES, P], BF16, name="bank")
        for s in (U, V):
            nc.tensor.transpose(gain_bank[:, s, :], gain_rows[:, s, :], identity[:])
        pack_w(nc.scalar.copy, "c", 1)
        for t in range(SLOTS):
            chains(U, t, 1)

        pack_w(nc.vector.tensor_copy, "c", 0)
        pack_w(nc.vector.tensor_copy, "b", 0)
        quantise_w("c", 0)
        nc.vector.tensor_copy(out=gain_cols[:].rearrange("p (s t) -> p s t", s=PHASES), in_=gain_bank[:, :, 0:SLOTS])
        quantise_w("b", 0)
        block(0)
        half_rows(0, IM, 0)
        negate_b(0)
        pack_uv(U, 1)
        quantise_w("nb", 0)
        half_rows(0, RE, 0)
        pack_uv(V, 1)
        quantise_uv(U, 1)
        quantise_uv(V, 1)
        half_rows(1, IM, 0)
        half_rows(1, RE, 0)
        for t in range(SLOTS):
            chains(V, t, 1)

        pack_w(nc.vector.tensor_copy, "b", 1)
        quantise_w("c", 1)
        quantise_w("b", 1)
        for m in (0, 1):
            half_rows(m, IM, 1)
        negate_b(1)
        times_gain(U, 1)
        quantise_w("nb", 1)
        for m in (0, 1):
            half_rows(m, RE, 1)
        times_gain(V, 1)
        pack_uv(U, 2)
        pack_uv(V, 2)
        quantise_uv(U, 2)
        quantise_uv(V, 2)
        for m in range(3, BLOCKS):
            block(m)

        for m in range(2, BLOCKS):
            first_copy = nc.scalar.copy if m < 6 else nc.vector.tensor_copy
            for part in (IM, RE):
                if (m, part) == (BLOCKS - 1, RE):
                    half_rows(m, part, 0, first_copy)
                    half_rows(m, part, 1)
                else:
                    product(m, part, 0, first_copy)
                    product(m, part, 1, nc.scalar.copy)
                    store(m, part, 0, ANTENNAS)
